import numpy as np
import ml_dtypes


def mxq(x, axis, fmt="e4m3"):
    dtype, down = {"e4m3": (ml_dtypes.float8_e4m3fn, 7), "e5m2": (ml_dtypes.float8_e5m2, 14)}[fmt]
    v = np.moveaxis(np.asarray(x, np.float32).astype(ml_dtypes.bfloat16).astype(np.float64), axis, -1)
    blocks = v.reshape(v.shape[:-1] + (-1, 32))
    amax = np.abs(blocks).max(-1, keepdims=True)
    byte = np.maximum(np.where(amax > 0, np.frexp(amax)[1] - 1 + 127, 0) - down, 1)
    scale = np.exp2(byte - 127.0)
    codes = (blocks / scale).astype(np.float32).astype(dtype).astype(np.float64)
    return np.moveaxis((codes * scale).reshape(v.shape), -1, axis)


WIDE = False


def mx_kscale(k):
    if not WIDE:
        return np.ones(k)
    levels = np.array([10, -10, 5, -5, 0])
    if k % 512:
        return np.exp2(np.random.permutation(np.resize(levels, k // 32))).repeat(32)
    a = np.empty((k // 512, 16))
    for p in range(k // 512):
        a[p, :8] = np.random.permutation(np.resize(levels, 8))
        for g in range(8):
            far = levels[np.abs(levels - a[p, g]) >= 10]
            a[p, g + 8] = far[np.random.randint(len(far))]
    return np.exp2(a.ravel()).repeat(32)


BF16 = ml_dtypes.bfloat16


def bf(x):
    return np.asarray(x, np.float32).astype(BF16)


def f64(x):
    return np.asarray(x).astype(np.float64)


E2M1 = np.array([0.0, 0.5, 1.0, 1.5, 2.0, 3.0, 4.0, 6.0, -0.0, -0.5, -1.0, -1.5, -2.0, -3.0, -4.0, -6.0])


def pack_weight(w, fmt):
    k, n = w.shape
    w = f64(bf(w)).reshape(k // 32, 32, n)
    amax = np.abs(w).max(1)
    if fmt == "e4m3":
        byte = np.frexp(amax)[1] - 1 + 127 - 7
    else:
        mant, ex = np.frexp(amax / 6.0)
        byte = np.where(mant > 0.5, ex, ex - 1) + 127
    byte = np.clip(np.where(amax > 0, byte, 1), 1, 254)
    scaled = (w * np.exp2(127.0 - byte)[:, None, :]).reshape(k, n).astype(np.float32)
    by_word = np.ascontiguousarray(scaled.reshape(k // 512, 128, 4, n).transpose(0, 1, 3, 2))
    if fmt == "e4m3":
        words = by_word.astype(ml_dtypes.float8_e4m3fn).view(np.uint8)
    else:
        c = by_word.astype(ml_dtypes.float4_e2m1fn).view(np.uint8) & 0xF
        words = c[..., 0::2] | (c[..., 1::2] << 4)
    return np.ascontiguousarray(words), np.ascontiguousarray(byte.astype(np.uint8).reshape(k // 512, 16, n))


def unpack_weight(words, scales, fmt):
    g, p, n, _ = words.shape
    if fmt == "e4m3":
        vals = np.ascontiguousarray(words).view(ml_dtypes.float8_e4m3fn).astype(np.float64)
    else:
        nib = np.empty((g, p, n, 4), np.uint8)
        nib[..., 0::2] = words & 0xF
        nib[..., 1::2] = words >> 4
        vals = E2M1[nib]
    vals = vals * np.repeat(np.exp2(scales.astype(np.float64) - 127.0), 8, axis=1)[..., None]
    return vals.transpose(0, 1, 3, 2).reshape(g * 512, n)
def pack4(w):
    words, scales = pack_weight(w, "e2m1")
    return words.reshape(words.shape[0], 128, -1), scales


def unpack4(words, scales):
    return unpack_weight(words.reshape(words.shape[0], 128, -1, 2), scales, "e2m1")


L, D, F, P = 128, 1024, 512, 128
F2 = 2 * F


def draw0():
    u = mx_kscale(D)
    t = mx_kscale(F2)
    s = bf(np.random.standard_normal((L, D)) * u)
    w1_words, w1_scales = pack4(np.random.standard_normal((D, F2)) / np.sqrt(D) / u[:, None])
    b1 = bf(np.random.standard_normal(F2) * 0.3)
    g = bf((1.0 + 0.1 * np.random.standard_normal(F2)) * t)
    wo_words, wo_scales = pack4(np.random.standard_normal((F2, P)) / np.sqrt(F2) / t[:, None])
    bo = bf(np.random.standard_normal(P) * 0.3)
    return {
        "s": s,
        "w1_words": w1_words,
        "w1_scales": w1_scales,
        "b1": b1,
        "g": g,
        "wo_words": wo_words,
        "wo_scales": wo_scales,
        "bo": bo,
    }


def core(s, w1_words, w1_scales, b1, g, wo_words, wo_scales, bo):
    h = (mxq(f64(s), 1, "e4m3") @ unpack4(w1_words, w1_scales)) + f64(b1)
    q = h[:, 0:F]
    k = h[:, F:F2]
    q_j = q[None, :, :]
    k_i = k[:, None, :]
    prod = q_j * k_i
    diff = q_j - k_i
    c = np.concatenate([prod, diff], axis=-1) * f64(g)
    return (mxq(c, 2, "e4m3") @ unpack4(wo_words, wo_scales)) + f64(bo)


def e4m3fn_bytes(y):
    return np.clip(np.asarray(y, np.float64), -448.0, 448.0).astype(np.float32).astype(ml_dtypes.float8_e4m3fn).view(np.uint8)


def e4m3fn_values(b):
    return np.asarray(b, np.uint8).view(ml_dtypes.float8_e4m3fn).astype(np.float64)


def setup_inputs():
    d = draw0()
    x0 = np.asarray(d['s']).astype(np.float64)
    s = (np.max(np.abs(x0), axis=(0,), keepdims=True) / 448.0).astype(np.float32)
    out = {}
    for k, v in d.items():
        if k == 's':
            out['s_bytes'] = e4m3fn_bytes(x0 / s.astype(np.float64))
            out['s_scale'] = s
        else:
            out[k] = v
    return out


def reference(s_bytes, s_scale, w1_words, w1_scales, b1, g, wo_words, wo_scales, bo):
    return core(e4m3fn_values(s_bytes) * s_scale.astype(np.float64), w1_words, w1_scales, b1, g, wo_words, wo_scales, bo)

@@ -1,0 +1,333 @@
+from contextlib import ExitStack
+
+import concourse.mybir as mybir
+from concourse.masks import make_identity
+
+L, D, F, C = 128, 1024, 512, 128
+FLOPS = 2 * L * D * 2 * F + 2 * L * L * 2 * F * C
+
+F32 = mybir.dt.float32
+BF16 = mybir.dt.bfloat16
+I32 = mybir.dt.int32
+U32 = mybir.dt.uint32
+U8 = mybir.dt.uint8
+FP8 = mybir.dt.float8_e4m3fn
+FP8X4 = mybir.dt.float8_e4m3fn_x4
+FP4X4 = mybir.dt.float4_e2m1fn_x4
+ALU = mybir.AluOpType
+ACT = mybir.ActivationFunctionType
+
+P = 128
+T = 4
+BANK = 512
+QUADS = 32
+GROUPS = 16
+ROWS = 8
+SCALAR_ROWS = 2
+EARLY = 10
+
+
+def tile_esmfoldsequencetopairproductdifference_w4_kernel(
+    tc, s_bytes, s_scale, w1_words, w1_scales, b1, g, wo_words, wo_scales, bo, out
+):
+    nc = tc.nc
+    with ExitStack() as ctx:
+        keep = ctx.enter_context(tc.tile_pool(name="keep", bufs=1))
+        work = ctx.enter_context(tc.tile_pool(name="work", bufs=2))
+        psum = ctx.enter_context(tc.psum_pool(name="psum", bufs=1))
+        ctx.enter_context(tc.manual_schedule())
+
+        def spare_bank():
+            return psum.tile([P, BANK], F32, name="spare", tag="spare", bufs=5)
+
+        w1_sc = keep.tile([P, 2, 2 * F], U8, align_bytes=64)
+        wo_sc = keep.tile([P, 2, C], U8, align_bytes=64)
+        nc.vector.memset(w1_sc[:].bitcast(I32), 0)
+        nc.vector.memset(wo_sc[:].bitcast(I32), 0)
+        ident = keep.tile([P, P], F32)
+        make_identity(nc, ident[:])
+
+        s_raw = keep.tile([P, D], U8)
+        nc.sync.dma_start(out=s_raw[:], in_=s_bytes)
+        s_sc = keep.tile([P, 2, T], F32)
+        nc.sync.dma_start(out=s_sc[:], in_=s_scale.rearrange("o (g p t) -> p (o g) t", p=P, t=T))
+        w1_w = keep.tile([P, 2, 4 * F], U8, align_bytes=64)
+        nc.sync.dma_start(out=w1_w[:].bitcast(I32), in_=w1_words.rearrange("g p n -> p g n").bitcast(I32))
+        for q in range(4):
+            nc.sync.dma_start(
+                out=w1_sc[32 * q : 32 * q + 4, :, :].bitcast(I32),
+                in_=w1_scales[:, 4 * q : 4 * q + 4, :].rearrange("g r n -> r g n").bitcast(I32),
+            )
+        b1_all = keep.tile([P, 2 * F], BF16)
+        nc.sync.dma_start(out=b1_all[:], in_=b1.partition_broadcast(P))
+        g_col = keep.tile([P, 2, T], BF16)
+        nc.sync.dma_start(out=g_col[:], in_=g.rearrange("(h p t) -> p h t", h=2, t=T))
+        g2_all = keep.tile([P, F], BF16)
+        nc.sync.dma_start(out=g2_all[:], in_=g[F : 2 * F].partition_broadcast(P))
+        wo_w = keep.tile([P, 2, 2 * C], U8, align_bytes=64)
+        nc.sync.dma_start(out=wo_w[:].bitcast(I32), in_=wo_words.rearrange("g p n -> p g n").bitcast(I32))
+        for q in range(4):
+            nc.sync.dma_start(
+                out=wo_sc[32 * q : 32 * q + 4, :, :].bitcast(I32),
+                in_=wo_scales[:, 4 * q : 4 * q + 4, :].rearrange("g r n -> r g n").bitcast(I32),
+            )
+        bo_all = keep.tile([P, C], BF16)
+        nc.sync.dma_start(out=bo_all[:], in_=bo.partition_broadcast(P))
+
+        g2_col = keep.tile([P, T], F32)
+        g2_neg = keep.tile([P, T], F32)
+        nc.scalar.activation(out=g2_col[:], in_=g_col[:, 1, :], func=ACT.Copy)
+        nc.scalar.activation(out=g2_neg[:], in_=g_col[:, 1, :], func=ACT.Copy, scale=-1.0)
+
+        s_wide = keep.tile([P, D], BF16)
+        nc.vector.tensor_copy(out=s_wide[:], in_=s_raw[:].bitcast(FP8))
+        s_words = s_wide[:].bitcast(F32)
+        s_turned = spare_bank()
+        for gi in range(2):
+            for u in range(2):
+                nc.tensor.transpose(
+                    s_turned[:, (2 * gi + u) * P : (2 * gi + u + 1) * P],
+                    s_words[:, 256 * gi + u : 256 * (gi + 1) : 2],
+                    ident[:],
+                )
+        s_in = keep.tile([P, 2, L * T], BF16, align_bytes=64)
+        for gi in range(2):
+            nc.vector.tensor_tensor(
+                out=s_in[:, gi, :].rearrange("p (n u e) -> p n u e", u=2, e=2),
+                in0=s_turned[:, 256 * gi : 256 * (gi + 1)].bitcast(BF16).rearrange("p (u n e) -> p n u e", u=2, e=2),
+                in1=s_sc[:, gi, :].rearrange("p (u e) -> p u e", u=2).unsqueeze(1).to_broadcast([P, L, 2, 2]),
+                op=ALU.mult,
+            )
+        s_codes = keep.tile([P, 2 * L], U32, align_bytes=64)
+        s_scales = keep.tile([P, 2 * L], U8, align_bytes=64)
+        nc.vector.quantize_mx(
+            out=s_codes[:].bitcast(FP8X4), scales=s_scales[:], in_=s_in[:].rearrange("p g n -> p (g n)")
+        )
+
+        h_sb = []
+        for half in (1, 0):
+            h_ps = spare_bank()
+            for gi in range(2):
+                nc.tensor.matmul_mx(
+                    out=h_ps[:],
+                    lhsT=s_codes[:, gi * L : (gi + 1) * L].bitcast(FP8X4),
+                    lhsT_scale=s_scales[:, gi * L : (gi + 1) * L],
+                    rhs=w1_w[:, gi, half * 2 * F : (half + 1) * 2 * F].bitcast(FP4X4),
+                    rhs_scale=w1_sc[:, gi, half * F : (half + 1) * F],
+                    start=(gi == 0),
+                    stop=(gi == 1),
+                )
+            h_half = keep.tile([P, T, P], F32, name="h%d" % half)
+            nc.vector.tensor_tensor(
+                out=h_half[:],
+                in0=h_ps[:].rearrange("n (p t) -> n t p", t=T),
+                in1=b1_all[:, half * F : (half + 1) * F].rearrange("n (p t) -> n t p", t=T),
+                op=ALU.add,
+            )
+            h_sb.append(h_half)
+        k_tok, q_tok = h_sb
+
+        g2_tp = g2_all[:].rearrange("n (p t) -> n t p", t=T)
+        kg_tok = keep.tile([P, T, P], F32)
+        nc.vector.scalar_tensor_tensor(out=kg_tok[:], in0=k_tok[:], scalar=-1.0, in1=g2_tp, op0=ALU.mult, op1=ALU.mult)
+        qg_tok = keep.tile([P, T, P], F32)
+        nc.vector.tensor_tensor(out=qg_tok[:], in0=q_tok[:], in1=g2_tp, op=ALU.mult)
+
+        flat = out.rearrange("i j c -> (i j c)")
+        row = L * C
+        k_park = flat[56 * row : 64 * row]
+        q_park = flat[28 * row : 32 * row]
+        for cp in range(2):
+            nc.sync.dma_start(
+                out=k_park[cp * 4 * row : (cp + 1) * 4 * row].rearrange("(t n p) -> n t p", t=T, p=P), in_=kg_tok[:]
+            )
+        nc.sync.dma_start(out=q_park.rearrange("(n t p) -> n t p", t=T, p=P), in_=qg_tok[:])
+
+        k_rows = k_park.rearrange("(r a p) -> r a p", r=32, p=P)
+        xk_early = keep.tile([P, EARLY - 2, P], F32)
+        xk_late = keep.tile([P, QUADS - EARLY, P], F32)
+        xq = keep.tile([P, 16, P], F32)
+        for jh in range(4):
+            nc.sync.dma_start(out=xk_early[32 * jh : 32 * jh + 32, :, :], in_=k_rows[:, 2:EARLY, :])
+        for ii in range(4):
+            nc.sync.dma_start(out=xq[ii:P:4, :, :], in_=q_park.rearrange("(b r p) -> r b p", r=32, p=P))
+        for jh in range(4):
+            nc.sync.dma_start(out=xk_late[32 * jh : 32 * jh + 32, :, :], in_=k_rows[:, EARLY:QUADS, :])
+
+        k_ps = spare_bank()
+        for t in range(T):
+            nc.tensor.transpose(k_ps[:, t * P : (t + 1) * P], k_tok[:, t, :], ident[:])
+        q_planes_ps = spare_bank()
+        for t in range(T):
+            nc.tensor.transpose(q_planes_ps[:, t * P : (t + 1) * P], q_tok[:, t, :], ident[:])
+        q_ps = psum.tile([P, BANK], F32, tag="q")
+        for t in range(T):
+            nc.tensor.transpose(q_ps[:].rearrange("p (j t) -> p t j", t=T)[:, t, :], q_tok[:, t, :], ident[:])
+
+        k_view = k_ps[:].rearrange("p (t i a) -> p a i t", t=T, i=4)
+        kg2_neg = keep.tile([P, 2, 4, T], F32)
+        nc.vector.tensor_tensor(
+            out=kg2_neg[:],
+            in0=k_view[:, 0:2, :, :],
+            in1=g2_neg[:].unsqueeze(1).unsqueeze(1).to_broadcast([P, 2, 4, T]),
+            op=ALU.mult,
+        )
+        kg1 = keep.tile([P, QUADS, 4, T], F32)
+        nc.vector.tensor_tensor(
+            out=kg1[:],
+            in0=k_view,
+            in1=g_col[:, 0, :].unsqueeze(1).unsqueeze(1).to_broadcast([P, QUADS, 4, T]),
+            op=ALU.mult,
+        )
+        kg1_rows = kg1[:].rearrange("p a i t -> p (a i) t")
+        kg2_rows = kg2_neg[:].rearrange("p a i t -> p (a i) t")
+        q_planes = keep.tile([P, T, L], F32)
+        nc.scalar.copy(out=q_planes[:].rearrange("p t j -> p (t j)"), in_=q_planes_ps[:])
+
+        def c_tile(tag):
+            return work.tile([P, ROWS * L * T], BF16, name=tag, tag=tag, align_bytes=64)
+
+        def scalar_pairs(n, r0, is_diff):
+            pairs = work.tile([P, 2, 2, L, 2], BF16, name="pairs", tag="pairs", bufs=3)
+            for r in range(2):
+                for t in range(T):
+                    dst = pairs[:, r, t // 2, :, t % 2]
+                    if is_diff:
+                        nc.scalar.activation(
+                            out=dst,
+                            in_=q_planes[:, t, :],
+                            func=ACT.Identity,
+                            scale=g2_col[:, t : t + 1],
+                            bias=kg2_rows[:, r0 + r, t : t + 1],
+                        )
+                    else:
+                        nc.scalar.activation(
+                            out=dst,
+                            in_=q_planes[:, t, :],
+                            func=ACT.Copy,
+                            scale=kg1_rows[:, ROWS * n + r0 + r, t : t + 1],
+                        )
+            return pairs
+
+        def scalar_join(pairs, c, r0):
+            nc.scalar.copy(
+                out=c[:, r0 * L * T : (r0 + 2) * L * T].bitcast(F32).rearrange("p (r j u) -> p r j u", r=2, u=2),
+                in_=pairs[:].rearrange("p r u j e -> p (r u j e)").bitcast(F32).rearrange("p (r u j) -> p r j u", r=2, u=2),
+            )
+
+        def vector_product(n, c, rows):
+            nc.vector.tensor_tensor(
+                out=c[:, 0 : rows * L * T].rearrange("p (r j t) -> p r j t", j=L, t=T),
+                in0=q_ps[:].rearrange("p (j t) -> p j t", t=T).unsqueeze(1).to_broadcast([P, rows, L, T]),
+                in1=kg1_rows[:, ROWS * n : ROWS * n + rows, :].unsqueeze(2).to_broadcast([P, rows, L, T]),
+                op=ALU.mult,
+            )
+
+        def diff_bank(n, c, idx):
+            a2, beta = divmod(idx, 4)
+            a = 2 * n + a2
+            xk = xk_early[:, a - 2, :] if a < EARLY else xk_late[:, a - EARLY, :]
+            bank = spare_bank()
+            for bb in range(4):
+                dst = bank[:, bb * P : (bb + 1) * P]
+                nc.tensor.matmul(dst, lhsT=xq[:, 4 * beta + bb, :], rhs=ident[:], start=True, stop=False, is_transpose=True)
+                nc.tensor.matmul(dst, lhsT=xk, rhs=ident[:], start=False, stop=True, is_transpose=True)
+            nc.scalar.copy(
+                out=c[:].rearrange("p (r j t) -> p r j t", j=L, t=T)[:, 4 * a2 : 4 * a2 + 4, 32 * beta : 32 * beta + 32, :],
+                in_=bank[:].rearrange("p (j t i) -> p i j t", t=T, i=4),
+            )
+
+        def code_tiles(tag):
+            codes = work.tile([P, ROWS * L], U32, name=tag + "_codes", tag=tag + "_codes", align_bytes=64)
+            scales = work.tile([P, ROWS * L], U8, name=tag + "_scales", tag=tag + "_scales", align_bytes=64)
+            return codes, scales
+
+        def quantise(c, tiles, r0, r1):
+            nc.vector.quantize_mx(
+                out=tiles[0][:, r0 * L : r1 * L].bitcast(FP8X4),
+                scales=tiles[1][:, r0 * L : r1 * L],
+                in_=c[:, r0 * L * T : r1 * L * T],
+            )
+
+        def project(prod, diff, a2, bank):
+            for ii in range(4):
+                cols = slice((4 * a2 + ii) * L, (4 * a2 + ii + 1) * L)
+                for gi, tiles in enumerate((prod, diff)):
+                    nc.tensor.matmul_mx(
+                        out=bank[:, ii * C : (ii + 1) * C],
+                        lhsT=tiles[0][:, cols].bitcast(FP8X4),
+                        lhsT_scale=tiles[1][:, cols],
+                        rhs=wo_w[:, gi, :].bitcast(FP4X4),
+                        rhs_scale=wo_sc[:, gi, :],
+                        start=(gi == 0),
+                        stop=(gi == 1),
+                    )
+
+        out_rows = out.rearrange("(i a) j c -> a j i c", a=QUADS)
+
+        def finish(a, bank):
+            res = work.tile([P, 4, C], F32, name="res", tag="res", bufs=4)
+            nc.vector.tensor_tensor(
+                out=res[:],
+                in0=bank[:].rearrange("p (i c) -> p i c", i=4),
+                in1=bo_all[:].unsqueeze(1).to_broadcast([P, 4, C]),
+                op=ALU.add,
+            )
+            nc.sync.dma_start(out=out_rows[a], in_=res[:])
+
+        def out_bank():
+            return psum.tile([P, BANK], F32, name="acc", tag="acc", bufs=2)
+
+        c_prod = {0: c_tile("c_prod"), 1: c_tile("c_prod")}
+        c_diff = {0: c_tile("c_diff"), 1: c_tile("c_diff")}
+        vector_product(0, c_prod[0], ROWS)
+        vector_product(1, c_prod[1], ROWS)
+        waiting = None
+        for r0 in range(0, ROWS, 2):
+            pairs = scalar_pairs(0, r0, True)
+            if waiting is not None:
+                scalar_join(waiting, c_diff[0], r0 - 2)
+            waiting = pairs
+        diff_bank(1, c_diff[1], 0)
+        scalar_join(waiting, c_diff[0], ROWS - 2)
+        for idx in range(1, 8):
+            diff_bank(1, c_diff[1], idx)
+        prod_q = code_tiles("prod")
+        diff_q = code_tiles("diff")
+        quantise(c_prod[0], prod_q, 0, ROWS)
+        quantise(c_diff[0], diff_q, 0, ROWS)
+
+        for n in range(1, GROUPS - 1):
+            banks = [out_bank(), out_bank()]
+            for a2 in range(2):
+                project(prod_q, diff_q, a2, banks[a2])
+            c_prod[n + 1] = c_tile("c_prod")
+            c_diff[n + 1] = c_tile("c_diff")
+            pairs = scalar_pairs(n + 1, ROWS - SCALAR_ROWS, False)
+            diff_bank(n + 1, c_diff[n + 1], 0)
+            scalar_join(pairs, c_prod[n + 1], ROWS - SCALAR_ROWS)
+            for idx in range(1, 8):
+                diff_bank(n + 1, c_diff[n + 1], idx)
+            vector_product(n + 1, c_prod[n + 1], ROWS - SCALAR_ROWS)
+            for a2 in range(2):
+                finish(2 * (n - 1) + a2, banks[a2])
+            prod_q = code_tiles("prod")
+            diff_q = code_tiles("diff")
+            quantise(c_prod[n], prod_q, 0, ROWS)
+            quantise(c_diff[n], diff_q, 0, ROWS)
+
+        n = GROUPS - 1
+        banks = [out_bank(), out_bank()]
+        for a2 in range(2):
+            project(prod_q, diff_q, a2, banks[a2])
+        prod_q = code_tiles("prod")
+        diff_q = code_tiles("diff")
+        quantise(c_prod[n], prod_q, 0, ROWS)
+        for a2 in range(2):
+            quantise(c_diff[n], diff_q, 4 * a2, 4 * a2 + 4)
+        for a2 in range(2):
+            finish(2 * (n - 1) + a2, banks[a2])
+        for a2 in range(2):
+            bank = spare_bank()
+            project(prod_q, diff_q, a2, bank)
+            finish(2 * n + a2, bank)

@@ -24,6 +24,9 @@ QUADS = 32
 GROUPS = 16
 ROWS = 8
 SCALAR_ROWS = 2
+GPSIMD_ROWS = 1
+VECTOR_ROWS = ROWS - SCALAR_ROWS - GPSIMD_ROWS
+BANKS = 3
 EARLY = 10
 
 
@@ -75,9 +78,7 @@ def tile_esmfoldsequencetopairproductdifference_w4_kernel(
         nc.sync.dma_start(out=bo_all[:], in_=bo.partition_broadcast(P))
 
         g2_col = keep.tile([P, T], F32)
-        g2_neg = keep.tile([P, T], F32)
         nc.scalar.activation(out=g2_col[:], in_=g_col[:, 1, :], func=ACT.Copy)
-        nc.scalar.activation(out=g2_neg[:], in_=g_col[:, 1, :], func=ACT.Copy, scale=-1.0)
 
         s_wide = keep.tile([P, D], BF16)
         nc.vector.tensor_copy(out=s_wide[:], in_=s_raw[:].bitcast(FP8))
@@ -146,43 +147,55 @@ def tile_esmfoldsequencetopairproductdifference_w4_kernel(
         k_rows = k_park.rearrange("(r a p) -> r a p", r=32, p=P)
         xk_early = keep.tile([P, EARLY - 2, P], F32)
         xk_late = keep.tile([P, QUADS - EARLY, P], F32)
-        xq = keep.tile([P, 16, P], F32)
+        xq = keep.tile([P, 4 * BANKS, P], F32)
         for jh in range(4):
             nc.sync.dma_start(out=xk_early[32 * jh : 32 * jh + 32, :, :], in_=k_rows[:, 2:EARLY, :])
         for ii in range(4):
-            nc.sync.dma_start(out=xq[ii:P:4, :, :], in_=q_park.rearrange("(b r p) -> r b p", r=32, p=P))
+            nc.sync.dma_start(out=xq[ii:P:4, :, :], in_=q_park.rearrange("(b r p) -> r b p", r=32, p=P)[:, 0 : 4 * BANKS, :])
         for jh in range(4):
             nc.sync.dma_start(out=xk_late[32 * jh : 32 * jh + 32, :, :], in_=k_rows[:, EARLY:QUADS, :])
 
-        k_ps = spare_bank()
-        for t in range(T):
-            nc.tensor.transpose(k_ps[:, t * P : (t + 1) * P], k_tok[:, t, :], ident[:])
-        q_planes_ps = spare_bank()
-        for t in range(T):
-            nc.tensor.transpose(q_planes_ps[:, t * P : (t + 1) * P], q_tok[:, t, :], ident[:])
-        q_ps = psum.tile([P, BANK], F32, tag="q")
-        for t in range(T):
-            nc.tensor.transpose(q_ps[:].rearrange("p (j t) -> p t j", t=T)[:, t, :], q_tok[:, t, :], ident[:])
+        def turn(tok, bank_view):
+            for t in range(T):
+                nc.tensor.transpose(bank_view[:, t, :], tok[:, t, :], ident[:])
 
-        k_view = k_ps[:].rearrange("p (t i a) -> p a i t", t=T, i=4)
-        kg2_neg = keep.tile([P, 2, 4, T], F32)
-        nc.vector.tensor_tensor(
-            out=kg2_neg[:],
-            in0=k_view[:, 0:2, :, :],
-            in1=g2_neg[:].unsqueeze(1).unsqueeze(1).to_broadcast([P, 2, 4, T]),
-            op=ALU.mult,
-        )
+        def turned(tok):
+            bank = spare_bank()
+            turn(tok, bank[:].rearrange("p (t n) -> p t n", t=T))
+            return bank
+
+        k_ps = turned(k_tok)
+        q_ps = psum.tile([P, BANK], F32, tag="q")
+        turn(q_tok, q_ps[:].rearrange("p (j t) -> p t j", t=T))
+        kg_ps = turned(kg_tok)
+        qg_ps = turned(qg_tok)
+        q_planes_ps = turned(q_tok)
+
         kg1 = keep.tile([P, QUADS, 4, T], F32)
         nc.vector.tensor_tensor(
             out=kg1[:],
-            in0=k_view,
+            in0=k_ps[:].rearrange("p (t i a) -> p a i t", t=T, i=4),
             in1=g_col[:, 0, :].unsqueeze(1).unsqueeze(1).to_broadcast([P, QUADS, 4, T]),
             op=ALU.mult,
         )
-        kg1_rows = kg1[:].rearrange("p a i t -> p (a i) t")
-        kg2_rows = kg2_neg[:].rearrange("p a i t -> p (a i) t")
+        kg2_neg = keep.tile([P, QUADS, 4, T], F32)
+        nc.scalar.copy(out=kg2_neg[:], in_=kg_ps[:].rearrange("p (t i a) -> p a i t", t=T, i=4))
+        qg2 = keep.tile([P, L, T], F32)
+        nc.scalar.copy(out=qg2[:], in_=qg_ps[:].rearrange("p (t j) -> p j t", t=T))
         q_planes = keep.tile([P, T, L], F32)
         nc.scalar.copy(out=q_planes[:].rearrange("p t j -> p (t j)"), in_=q_planes_ps[:])
+        kg1_rows = kg1[:].rearrange("p a i t -> p (a i) t")
+        kg2_rows = kg2_neg[:].rearrange("p a i t -> p (a i) t")
+        q_sb = keep.tile([P, L, T], F32)
+
+        def gpsimd_part(c, op, q_side, k_rows_side, n, r0, r1, j0):
+            shape = [P, r1 - r0, L - j0, T]
+            nc.gpsimd.tensor_tensor(
+                out=c[:].rearrange("p (r j t) -> p r j t", j=L, t=T)[:, r0:r1, j0:L, :],
+                in0=q_side[:, j0:L, :].unsqueeze(1).to_broadcast(shape),
+                in1=k_rows_side[:, ROWS * n + r0 : ROWS * n + r1, :].unsqueeze(2).to_broadcast(shape),
+                op=op,
+            )
 
         def c_tile(tag):
             return work.tile([P, ROWS * L * T], BF16, name=tag, tag=tag, align_bytes=64)
@@ -224,7 +237,7 @@ def tile_esmfoldsequencetopairproductdifference_w4_kernel(
             )
 
         def diff_bank(n, c, idx):
-            a2, beta = divmod(idx, 4)
+            a2, beta = divmod(idx, BANKS)
             a = 2 * n + a2
             xk = xk_early[:, a - 2, :] if a < EARLY else xk_late[:, a - EARLY, :]
             bank = spare_bank()
@@ -281,16 +294,18 @@ def tile_esmfoldsequencetopairproductdifference_w4_kernel(
         c_prod = {0: c_tile("c_prod"), 1: c_tile("c_prod")}
         c_diff = {0: c_tile("c_diff"), 1: c_tile("c_diff")}
         vector_product(0, c_prod[0], ROWS)
-        vector_product(1, c_prod[1], ROWS)
-        waiting = None
-        for r0 in range(0, ROWS, 2):
-            pairs = scalar_pairs(0, r0, True)
-            if waiting is not None:
-                scalar_join(waiting, c_diff[0], r0 - 2)
-            waiting = pairs
+        vector_product(1, c_prod[1], ROWS - SCALAR_ROWS)
+        gpsimd_part(c_diff[0], ALU.add, qg2, kg2_rows, 0, 4, ROWS, 0)
+        gpsimd_part(c_diff[1], ALU.add, qg2, kg2_rows, 1, 0, ROWS, 32 * BANKS)
+        first = scalar_pairs(0, 0, True)
+        second = scalar_pairs(0, 2, True)
+        scalar_join(first, c_diff[0], 0)
+        nc.scalar.copy(out=q_sb[:], in_=q_planes_ps[:].rearrange("p (t j) -> p j t", t=T))
+        scalar_join(second, c_diff[0], 2)
+        pairs = scalar_pairs(1, ROWS - SCALAR_ROWS, False)
         diff_bank(1, c_diff[1], 0)
-        scalar_join(waiting, c_diff[0], ROWS - 2)
-        for idx in range(1, 8):
+        scalar_join(pairs, c_prod[1], ROWS - SCALAR_ROWS)
+        for idx in range(1, 2 * BANKS):
             diff_bank(1, c_diff[1], idx)
         prod_q = code_tiles("prod")
         diff_q = code_tiles("diff")
@@ -303,12 +318,14 @@ def tile_esmfoldsequencetopairproductdifference_w4_kernel(
                 project(prod_q, diff_q, a2, banks[a2])
             c_prod[n + 1] = c_tile("c_prod")
             c_diff[n + 1] = c_tile("c_diff")
+            gpsimd_part(c_prod[n + 1], ALU.mult, q_sb, kg1_rows, n + 1, VECTOR_ROWS, VECTOR_ROWS + GPSIMD_ROWS, 0)
+            gpsimd_part(c_diff[n + 1], ALU.add, qg2, kg2_rows, n + 1, 0, ROWS, 32 * BANKS)
             pairs = scalar_pairs(n + 1, ROWS - SCALAR_ROWS, False)
             diff_bank(n + 1, c_diff[n + 1], 0)
             scalar_join(pairs, c_prod[n + 1], ROWS - SCALAR_ROWS)
-            for idx in range(1, 8):
+            for idx in range(1, 2 * BANKS):
                 diff_bank(n + 1, c_diff[n + 1], idx)
-            vector_product(n + 1, c_prod[n + 1], ROWS - SCALAR_ROWS)
+            vector_product(n + 1, c_prod[n + 1], VECTOR_ROWS)
             for a2 in range(2):
                 finish(2 * (n - 1) + a2, banks[a2])
             prod_q = code_tiles("prod")

@@ -24,9 +24,10 @@ QUADS = 32
 GROUPS = 16
 ROWS = 8
 SCALAR_ROWS = 2
-GPSIMD_ROWS = 1
-VECTOR_ROWS = ROWS - SCALAR_ROWS - GPSIMD_ROWS
-BANKS = 3
+SHARED_ROWS = ROWS - SCALAR_ROWS
+PROD_J = 96
+DIFF_J = 104
+TILES = DIFF_J // 8
 EARLY = 10
 
 
@@ -54,19 +55,25 @@ def tile_esmfoldsequencetopairproductdifference_w4_kernel(
         nc.sync.dma_start(out=s_raw[:], in_=s_bytes)
         s_sc = keep.tile([P, 2, T], F32)
         nc.sync.dma_start(out=s_sc[:], in_=s_scale.rearrange("o (g p t) -> p (o g) t", p=P, t=T))
-        w1_w = keep.tile([P, 2, 4 * F], U8, align_bytes=64)
-        nc.sync.dma_start(out=w1_w[:].bitcast(I32), in_=w1_words.rearrange("g p n -> p g n").bitcast(I32))
+        w1_w = [keep.tile([P, 2, 2 * F], U8, align_bytes=64, name="w1_w%d" % half) for half in range(2)]
+        w1_src = w1_words.rearrange("g p n -> p g n")
+
+        def load_w1(half):
+            nc.sync.dma_start(
+                out=w1_w[half][:].bitcast(I32), in_=w1_src[:, :, half * 2 * F : (half + 1) * 2 * F].bitcast(I32)
+            )
+
+        load_w1(1)
         for q in range(4):
             nc.sync.dma_start(
                 out=w1_sc[32 * q : 32 * q + 4, :, :].bitcast(I32),
                 in_=w1_scales[:, 4 * q : 4 * q + 4, :].rearrange("g r n -> r g n").bitcast(I32),
             )
-        b1_all = keep.tile([P, 2 * F], BF16)
-        nc.sync.dma_start(out=b1_all[:], in_=b1.partition_broadcast(P))
-        g_col = keep.tile([P, 2, T], BF16)
-        nc.sync.dma_start(out=g_col[:], in_=g.rearrange("(h p t) -> p h t", h=2, t=T))
-        g2_all = keep.tile([P, F], BF16)
-        nc.sync.dma_start(out=g2_all[:], in_=g[F : 2 * F].partition_broadcast(P))
+        b1_raw = keep.tile([P, 2, T], BF16)
+        nc.sync.dma_start(out=b1_raw[:], in_=b1.rearrange("(h p t) -> p h t", h=2, t=T))
+        g_raw = keep.tile([P, 2, T], BF16)
+        nc.sync.dma_start(out=g_raw[:], in_=g.rearrange("(h p t) -> p h t", h=2, t=T))
+        load_w1(0)
         wo_w = keep.tile([P, 2, 2 * C], U8, align_bytes=64)
         nc.sync.dma_start(out=wo_w[:].bitcast(I32), in_=wo_words.rearrange("g p n -> p g n").bitcast(I32))
         for q in range(4):
@@ -77,8 +84,10 @@ def tile_esmfoldsequencetopairproductdifference_w4_kernel(
         bo_all = keep.tile([P, C], BF16)
         nc.sync.dma_start(out=bo_all[:], in_=bo.partition_broadcast(P))
 
-        g2_col = keep.tile([P, T], F32)
-        nc.scalar.activation(out=g2_col[:], in_=g_col[:, 1, :], func=ACT.Copy)
+        b1_col = keep.tile([P, 2, T], F32)
+        nc.scalar.activation(out=b1_col[:], in_=b1_raw[:], func=ACT.Copy)
+        g_col = keep.tile([P, 2, T], F32)
+        nc.scalar.activation(out=g_col[:], in_=g_raw[:], func=ACT.Copy)
 
         s_wide = keep.tile([P, D], BF16)
         nc.vector.tensor_copy(out=s_wide[:], in_=s_raw[:].bitcast(FP8))
@@ -91,6 +100,18 @@ def tile_esmfoldsequencetopairproductdifference_w4_kernel(
                     s_words[:, 256 * gi + u : 256 * (gi + 1) : 2],
                     ident[:],
                 )
+
+        def spread(col, name):
+            bank = spare_bank()
+            for t in range(T):
+                nc.tensor.transpose(bank[:, t * P : (t + 1) * P], col[:, t : t + 1].to_broadcast([P, P]), ident[:])
+            wide = keep.tile([P, T, P], F32, name=name)
+            nc.scalar.copy(out=wide[:].rearrange("n t p -> n (t p)"), in_=bank[:])
+            return wide
+
+        b1_k = spread(b1_col[:, 1, :], "b1_k")
+        b1_q = spread(b1_col[:, 0, :], "b1_q")
+        g2_all = spread(g_col[:, 1, :], "g2_all")
         s_in = keep.tile([P, 2, L * T], BF16, align_bytes=64)
         for gi in range(2):
             nc.vector.tensor_tensor(
@@ -106,14 +127,14 @@ def tile_esmfoldsequencetopairproductdifference_w4_kernel(
         )
 
         h_sb = []
-        for half in (1, 0):
+        for half, bias in ((1, b1_k), (0, b1_q)):
             h_ps = spare_bank()
             for gi in range(2):
                 nc.tensor.matmul_mx(
                     out=h_ps[:],
                     lhsT=s_codes[:, gi * L : (gi + 1) * L].bitcast(FP8X4),
                     lhsT_scale=s_scales[:, gi * L : (gi + 1) * L],
-                    rhs=w1_w[:, gi, half * 2 * F : (half + 1) * 2 * F].bitcast(FP4X4),
+                    rhs=w1_w[half][:, gi, :].bitcast(FP4X4),
                     rhs_scale=w1_sc[:, gi, half * F : (half + 1) * F],
                     start=(gi == 0),
                     stop=(gi == 1),
@@ -122,13 +143,13 @@ def tile_esmfoldsequencetopairproductdifference_w4_kernel(
             nc.vector.tensor_tensor(
                 out=h_half[:],
                 in0=h_ps[:].rearrange("n (p t) -> n t p", t=T),
-                in1=b1_all[:, half * F : (half + 1) * F].rearrange("n (p t) -> n t p", t=T),
+                in1=bias[:],
                 op=ALU.add,
             )
             h_sb.append(h_half)
         k_tok, q_tok = h_sb
 
-        g2_tp = g2_all[:].rearrange("n (p t) -> n t p", t=T)
+        g2_tp = g2_all[:]
         kg_tok = keep.tile([P, T, P], F32)
         nc.vector.scalar_tensor_tensor(out=kg_tok[:], in0=k_tok[:], scalar=-1.0, in1=g2_tp, op0=ALU.mult, op1=ALU.mult)
         qg_tok = keep.tile([P, T, P], F32)
@@ -147,11 +168,11 @@ def tile_esmfoldsequencetopairproductdifference_w4_kernel(
         k_rows = k_park.rearrange("(r a p) -> r a p", r=32, p=P)
         xk_early = keep.tile([P, EARLY - 2, P], F32)
         xk_late = keep.tile([P, QUADS - EARLY, P], F32)
-        xq = keep.tile([P, 4 * BANKS, P], F32)
+        xq = keep.tile([P, TILES, P], F32)
         for jh in range(4):
             nc.sync.dma_start(out=xk_early[32 * jh : 32 * jh + 32, :, :], in_=k_rows[:, 2:EARLY, :])
         for ii in range(4):
-            nc.sync.dma_start(out=xq[ii:P:4, :, :], in_=q_park.rearrange("(b r p) -> r b p", r=32, p=P)[:, 0 : 4 * BANKS, :])
+            nc.sync.dma_start(out=xq[ii:P:4, :, :], in_=q_park.rearrange("(b r p) -> r b p", r=32, p=P)[:, 0:TILES, :])
         for jh in range(4):
             nc.sync.dma_start(out=xk_late[32 * jh : 32 * jh + 32, :, :], in_=k_rows[:, EARLY:QUADS, :])
 
@@ -210,7 +231,7 @@ def tile_esmfoldsequencetopairproductdifference_w4_kernel(
                             out=dst,
                             in_=q_planes[:, t, :],
                             func=ACT.Identity,
-                            scale=g2_col[:, t : t + 1],
+                            scale=g_col[:, 1, t : t + 1],
                             bias=kg2_rows[:, r0 + r, t : t + 1],
                         )
                     else:
@@ -228,27 +249,38 @@ def tile_esmfoldsequencetopairproductdifference_w4_kernel(
                 in_=pairs[:].rearrange("p r u j e -> p (r u j e)").bitcast(F32).rearrange("p (r u j) -> p r j u", r=2, u=2),
             )
 
-        def vector_product(n, c, rows):
+        def vector_product(n, c, rows, cols):
+            shape = [P, rows, cols, T]
             nc.vector.tensor_tensor(
-                out=c[:, 0 : rows * L * T].rearrange("p (r j t) -> p r j t", j=L, t=T),
-                in0=q_ps[:].rearrange("p (j t) -> p j t", t=T).unsqueeze(1).to_broadcast([P, rows, L, T]),
-                in1=kg1_rows[:, ROWS * n : ROWS * n + rows, :].unsqueeze(2).to_broadcast([P, rows, L, T]),
+                out=c[:].rearrange("p (r j t) -> p r j t", j=L, t=T)[:, 0:rows, 0:cols, :],
+                in0=q_ps[:].rearrange("p (j t) -> p j t", t=T)[:, 0:cols, :].unsqueeze(1).to_broadcast(shape),
+                in1=kg1_rows[:, ROWS * n : ROWS * n + rows, :].unsqueeze(2).to_broadcast(shape),
                 op=ALU.mult,
             )
 
-        def diff_bank(n, c, idx):
-            a2, beta = divmod(idx, BANKS)
-            a = 2 * n + a2
+        def diff_tile(dst, a, b):
             xk = xk_early[:, a - 2, :] if a < EARLY else xk_late[:, a - EARLY, :]
+            nc.tensor.matmul(dst, lhsT=xq[:, b, :], rhs=ident[:], start=True, stop=False, is_transpose=True)
+            nc.tensor.matmul(dst, lhsT=xk, rhs=ident[:], start=False, stop=True, is_transpose=True)
+
+        def diff_bank(n, c, idx):
             bank = spare_bank()
-            for bb in range(4):
-                dst = bank[:, bb * P : (bb + 1) * P]
-                nc.tensor.matmul(dst, lhsT=xq[:, 4 * beta + bb, :], rhs=ident[:], start=True, stop=False, is_transpose=True)
-                nc.tensor.matmul(dst, lhsT=xk, rhs=ident[:], start=False, stop=True, is_transpose=True)
-            nc.scalar.copy(
-                out=c[:].rearrange("p (r j t) -> p r j t", j=L, t=T)[:, 4 * a2 : 4 * a2 + 4, 32 * beta : 32 * beta + 32, :],
-                in_=bank[:].rearrange("p (j t i) -> p i j t", t=T, i=4),
-            )
+            c_rows = c[:].rearrange("p (a i j t) -> p a i j t", i=4, j=L, t=T)
+            if idx > 0:
+                a2, beta = divmod(idx - 1, 3)
+                for bb in range(4):
+                    diff_tile(bank[:, bb * P : (bb + 1) * P], 2 * n + a2, 4 * beta + bb)
+                nc.scalar.copy(
+                    out=c_rows[:, a2, :, 32 * beta : 32 * beta + 32, :],
+                    in_=bank[:].rearrange("p (j t i) -> p i j t", t=T, i=4),
+                )
+            else:
+                for a2 in range(2):
+                    diff_tile(bank[:, a2 * P : (a2 + 1) * P], 2 * n + a2, TILES - 1)
+                nc.scalar.copy(
+                    out=c_rows[:, :, :, 96:DIFF_J, :],
+                    in_=bank[:, 0 : 2 * P].rearrange("p (a j t i) -> p a i j t", a=2, t=T, i=4),
+                )
 
         def code_tiles(tag):
             codes = work.tile([P, ROWS * L], U32, name=tag + "_codes", tag=tag + "_codes", align_bytes=64)
@@ -293,10 +325,10 @@ def tile_esmfoldsequencetopairproductdifference_w4_kernel(
 
         c_prod = {0: c_tile("c_prod"), 1: c_tile("c_prod")}
         c_diff = {0: c_tile("c_diff"), 1: c_tile("c_diff")}
-        vector_product(0, c_prod[0], ROWS)
-        vector_product(1, c_prod[1], ROWS - SCALAR_ROWS)
+        vector_product(0, c_prod[0], ROWS, L)
+        vector_product(1, c_prod[1], SHARED_ROWS, L)
         gpsimd_part(c_diff[0], ALU.add, qg2, kg2_rows, 0, 4, ROWS, 0)
-        gpsimd_part(c_diff[1], ALU.add, qg2, kg2_rows, 1, 0, ROWS, 32 * BANKS)
+        gpsimd_part(c_diff[1], ALU.add, qg2, kg2_rows, 1, 0, ROWS, DIFF_J)
         first = scalar_pairs(0, 0, True)
         second = scalar_pairs(0, 2, True)
         scalar_join(first, c_diff[0], 0)
@@ -305,7 +337,7 @@ def tile_esmfoldsequencetopairproductdifference_w4_kernel(
         pairs = scalar_pairs(1, ROWS - SCALAR_ROWS, False)
         diff_bank(1, c_diff[1], 0)
         scalar_join(pairs, c_prod[1], ROWS - SCALAR_ROWS)
-        for idx in range(1, 2 * BANKS):
+        for idx in range(1, 7):
             diff_bank(1, c_diff[1], idx)
         prod_q = code_tiles("prod")
         diff_q = code_tiles("diff")
@@ -318,14 +350,14 @@ def tile_esmfoldsequencetopairproductdifference_w4_kernel(
                 project(prod_q, diff_q, a2, banks[a2])
             c_prod[n + 1] = c_tile("c_prod")
             c_diff[n + 1] = c_tile("c_diff")
-            gpsimd_part(c_prod[n + 1], ALU.mult, q_sb, kg1_rows, n + 1, VECTOR_ROWS, VECTOR_ROWS + GPSIMD_ROWS, 0)
-            gpsimd_part(c_diff[n + 1], ALU.add, qg2, kg2_rows, n + 1, 0, ROWS, 32 * BANKS)
+            gpsimd_part(c_prod[n + 1], ALU.mult, q_sb, kg1_rows, n + 1, 0, SHARED_ROWS, PROD_J)
+            gpsimd_part(c_diff[n + 1], ALU.add, qg2, kg2_rows, n + 1, 0, ROWS, DIFF_J)
             pairs = scalar_pairs(n + 1, ROWS - SCALAR_ROWS, False)
             diff_bank(n + 1, c_diff[n + 1], 0)
             scalar_join(pairs, c_prod[n + 1], ROWS - SCALAR_ROWS)
-            for idx in range(1, 2 * BANKS):
+            for idx in range(1, 7):
                 diff_bank(n + 1, c_diff[n + 1], idx)
-            vector_product(n + 1, c_prod[n + 1], VECTOR_ROWS)
+            vector_product(n + 1, c_prod[n + 1], SHARED_ROWS, PROD_J)
             for a2 in range(2):
                 finish(2 * (n - 1) + a2, banks[a2])
             prod_q = code_tiles("prod")

@@ -28,7 +28,8 @@ SHARED_ROWS = ROWS - SCALAR_ROWS
 PROD_J = 96
 DIFF_J = 104
 TILES = DIFF_J // 8
-EARLY = 10
+K_CUTS = (2, 4, 12, QUADS)
+Q_CUTS = (0, 4, TILES)
 
 
 def tile_esmfoldsequencetopairproductdifference_w4_kernel(
@@ -50,6 +51,12 @@ def tile_esmfoldsequencetopairproductdifference_w4_kernel(
         nc.vector.memset(wo_sc[:].bitcast(I32), 0)
         ident = keep.tile([P, P], F32)
         make_identity(nc, ident[:])
+        ident_bf = keep.tile([P, P], BF16)
+        nc.vector.tensor_copy(out=ident_bf[:], in_=ident[:])
+        b1_raw = keep.tile([P, 2, T], BF16)
+        nc.scalar.dma_start(out=b1_raw[:], in_=b1.rearrange("(h p t) -> p h t", h=2, t=T))
+        g_raw = keep.tile([P, 2, T], BF16)
+        nc.scalar.dma_start(out=g_raw[:], in_=g.rearrange("(h p t) -> p h t", h=2, t=T))
 
         s_raw = keep.tile([P, D], U8)
         nc.sync.dma_start(out=s_raw[:], in_=s_bytes)
@@ -69,10 +76,6 @@ def tile_esmfoldsequencetopairproductdifference_w4_kernel(
                 out=w1_sc[32 * q : 32 * q + 4, :, :].bitcast(I32),
                 in_=w1_scales[:, 4 * q : 4 * q + 4, :].rearrange("g r n -> r g n").bitcast(I32),
             )
-        b1_raw = keep.tile([P, 2, T], BF16)
-        nc.sync.dma_start(out=b1_raw[:], in_=b1.rearrange("(h p t) -> p h t", h=2, t=T))
-        g_raw = keep.tile([P, 2, T], BF16)
-        nc.sync.dma_start(out=g_raw[:], in_=g.rearrange("(h p t) -> p h t", h=2, t=T))
         load_w1(0)
         wo_w = keep.tile([P, 2, 2 * C], U8, align_bytes=64)
         nc.sync.dma_start(out=wo_w[:].bitcast(I32), in_=wo_words.rearrange("g p n -> p g n").bitcast(I32))
@@ -84,47 +87,56 @@ def tile_esmfoldsequencetopairproductdifference_w4_kernel(
         bo_all = keep.tile([P, C], BF16)
         nc.sync.dma_start(out=bo_all[:], in_=bo.partition_broadcast(P))
 
-        b1_col = keep.tile([P, 2, T], F32)
-        nc.scalar.activation(out=b1_col[:], in_=b1_raw[:], func=ACT.Copy)
         g_col = keep.tile([P, 2, T], F32)
         nc.scalar.activation(out=g_col[:], in_=g_raw[:], func=ACT.Copy)
 
-        s_wide = keep.tile([P, D], BF16)
-        nc.vector.tensor_copy(out=s_wide[:], in_=s_raw[:].bitcast(FP8))
-        s_words = s_wide[:].bitcast(F32)
-        s_turned = spare_bank()
-        for gi in range(2):
-            for u in range(2):
-                nc.tensor.transpose(
-                    s_turned[:, (2 * gi + u) * P : (2 * gi + u + 1) * P],
-                    s_words[:, 256 * gi + u : 256 * (gi + 1) : 2],
-                    ident[:],
-                )
-
-        def spread(col, name):
+        def spread(col):
             bank = spare_bank()
             for t in range(T):
-                nc.tensor.transpose(bank[:, t * P : (t + 1) * P], col[:, t : t + 1].to_broadcast([P, P]), ident[:])
+                nc.tensor.matmul(
+                    bank[:, t * P : (t + 1) * P],
+                    lhsT=col[:, t : t + 1].to_broadcast([P, P]),
+                    rhs=ident_bf[:],
+                    start=True,
+                    stop=True,
+                )
+            return bank
+
+        def emptied(bank, name, scale):
             wide = keep.tile([P, T, P], F32, name=name)
-            nc.scalar.copy(out=wide[:].rearrange("n t p -> n (t p)"), in_=bank[:])
+            nc.scalar.activation(out=wide[:].rearrange("n t p -> n (t p)"), in_=bank[:], func=ACT.Copy, scale=scale)
             return wide
 
-        b1_k = spread(b1_col[:, 1, :], "b1_k")
-        b1_q = spread(b1_col[:, 0, :], "b1_q")
-        g2_all = spread(g_col[:, 1, :], "g2_all")
+        b1_k = emptied(spread(b1_raw[:, 1, :]), "b1_k", 1.0)
+        b1_q = emptied(spread(b1_raw[:, 0, :]), "b1_q", 1.0)
+
+        s_turned = []
+        for gi in range(2):
+            s_wide = keep.tile([P, BANK], BF16, name="s_wide%d" % gi)
+            nc.vector.tensor_copy(out=s_wide[:], in_=s_raw[:, gi * BANK : (gi + 1) * BANK].bitcast(FP8))
+            bank = spare_bank()
+            for u in range(2):
+                nc.tensor.transpose(bank[:, u * P : (u + 1) * P], s_wide[:].bitcast(F32)[:, u:256:2], ident[:])
+            s_turned.append(bank)
+        g2_ps = spread(g_raw[:, 1, :])
+        g2_neg = emptied(g2_ps, "g2_neg", -1.0)
+        g2_all = emptied(g2_ps, "g2_all", 1.0)
         s_in = keep.tile([P, 2, L * T], BF16, align_bytes=64)
         for gi in range(2):
             nc.vector.tensor_tensor(
                 out=s_in[:, gi, :].rearrange("p (n u e) -> p n u e", u=2, e=2),
-                in0=s_turned[:, 256 * gi : 256 * (gi + 1)].bitcast(BF16).rearrange("p (u n e) -> p n u e", u=2, e=2),
+                in0=s_turned[gi][:, 0:256].bitcast(BF16).rearrange("p (u n e) -> p n u e", u=2, e=2),
                 in1=s_sc[:, gi, :].rearrange("p (u e) -> p u e", u=2).unsqueeze(1).to_broadcast([P, L, 2, 2]),
                 op=ALU.mult,
             )
         s_codes = keep.tile([P, 2 * L], U32, align_bytes=64)
         s_scales = keep.tile([P, 2 * L], U8, align_bytes=64)
-        nc.vector.quantize_mx(
-            out=s_codes[:].bitcast(FP8X4), scales=s_scales[:], in_=s_in[:].rearrange("p g n -> p (g n)")
-        )
+        for gi in range(2):
+            nc.vector.quantize_mx(
+                out=s_codes[:, gi * L : (gi + 1) * L].bitcast(FP8X4),
+                scales=s_scales[:, gi * L : (gi + 1) * L],
+                in_=s_in[:, gi, :],
+            )
 
         h_sb = []
         for half, bias in ((1, b1_k), (0, b1_q)):
@@ -149,11 +161,28 @@ def tile_esmfoldsequencetopairproductdifference_w4_kernel(
             h_sb.append(h_half)
         k_tok, q_tok = h_sb
 
-        g2_tp = g2_all[:]
         kg_tok = keep.tile([P, T, P], F32)
-        nc.vector.scalar_tensor_tensor(out=kg_tok[:], in0=k_tok[:], scalar=-1.0, in1=g2_tp, op0=ALU.mult, op1=ALU.mult)
+        nc.gpsimd.tensor_tensor(out=kg_tok[:], in0=k_tok[:], in1=g2_neg[:], op=ALU.mult)
+
+        def turn(tok, bank_view):
+            for t in range(T):
+                nc.tensor.transpose(bank_view[:, t, :], tok[:, t, :], ident[:])
+
+        def turned(tok):
+            bank = spare_bank()
+            turn(tok, bank[:].rearrange("p (t n) -> p t n", t=T))
+            return bank
+
+        k_ps = turned(k_tok)
+        kg1 = keep.tile([P, QUADS, 4, T], F32)
+        nc.vector.tensor_tensor(
+            out=kg1[:],
+            in0=k_ps[:].rearrange("p (t i a) -> p a i t", t=T, i=4),
+            in1=g_col[:, 0, :].unsqueeze(1).unsqueeze(1).to_broadcast([P, QUADS, 4, T]),
+            op=ALU.mult,
+        )
         qg_tok = keep.tile([P, T, P], F32)
-        nc.vector.tensor_tensor(out=qg_tok[:], in0=q_tok[:], in1=g2_tp, op=ALU.mult)
+        nc.vector.tensor_tensor(out=qg_tok[:], in0=q_tok[:], in1=g2_all[:], op=ALU.mult)
 
         flat = out.rearrange("i j c -> (i j c)")
         row = L * C
@@ -166,45 +195,44 @@ def tile_esmfoldsequencetopairproductdifference_w4_kernel(
         nc.sync.dma_start(out=q_park.rearrange("(n t p) -> n t p", t=T, p=P), in_=qg_tok[:])
 
         k_rows = k_park.rearrange("(r a p) -> r a p", r=32, p=P)
-        xk_early = keep.tile([P, EARLY - 2, P], F32)
-        xk_late = keep.tile([P, QUADS - EARLY, P], F32)
-        xq = keep.tile([P, TILES, P], F32)
-        for jh in range(4):
-            nc.sync.dma_start(out=xk_early[32 * jh : 32 * jh + 32, :, :], in_=k_rows[:, 2:EARLY, :])
-        for ii in range(4):
-            nc.sync.dma_start(out=xq[ii:P:4, :, :], in_=q_park.rearrange("(b r p) -> r b p", r=32, p=P)[:, 0:TILES, :])
-        for jh in range(4):
-            nc.sync.dma_start(out=xk_late[32 * jh : 32 * jh + 32, :, :], in_=k_rows[:, EARLY:QUADS, :])
+        q_rows = q_park.rearrange("(b r p) -> r b p", r=32, p=P)
+        xk = {}
+        xq = {}
 
-        def turn(tok, bank_view):
-            for t in range(T):
-                nc.tensor.transpose(bank_view[:, t, :], tok[:, t, :], ident[:])
+        def load_k(piece):
+            a0, a1 = K_CUTS[piece], K_CUTS[piece + 1]
+            tiles = keep.tile([P, a1 - a0, P], F32, name="xk%d" % piece)
+            for jh in (0, 2, 1, 3):
+                nc.sync.dma_start(out=tiles[32 * jh : 32 * jh + 32, :, :], in_=k_rows[:, a0:a1, :])
+            for a in range(a0, a1):
+                xk[a] = tiles[:, a - a0, :]
 
-        def turned(tok):
-            bank = spare_bank()
-            turn(tok, bank[:].rearrange("p (t n) -> p t n", t=T))
-            return bank
+        def load_q(piece):
+            b0, b1_ = Q_CUTS[piece], Q_CUTS[piece + 1]
+            tiles = keep.tile([P, b1_ - b0, P], F32, name="xq%d" % piece)
+            for ii in range(4):
+                nc.sync.dma_start(out=tiles[ii:P:4, :, :], in_=q_rows[:, b0:b1_, :])
+            for b in range(b0, b1_):
+                xq[b] = tiles[:, b - b0, :]
 
-        k_ps = turned(k_tok)
+        load_k(0)
+        load_q(0)
+        load_q(1)
+        load_k(1)
+        load_k(2)
+
         q_ps = psum.tile([P, BANK], F32, tag="q")
         turn(q_tok, q_ps[:].rearrange("p (j t) -> p t j", t=T))
+        q_planes_ps = turned(q_tok)
         kg_ps = turned(kg_tok)
         qg_ps = turned(qg_tok)
-        q_planes_ps = turned(q_tok)
 
-        kg1 = keep.tile([P, QUADS, 4, T], F32)
-        nc.vector.tensor_tensor(
-            out=kg1[:],
-            in0=k_ps[:].rearrange("p (t i a) -> p a i t", t=T, i=4),
-            in1=g_col[:, 0, :].unsqueeze(1).unsqueeze(1).to_broadcast([P, QUADS, 4, T]),
-            op=ALU.mult,
-        )
+        q_planes = keep.tile([P, T, L], F32)
+        nc.scalar.copy(out=q_planes[:].rearrange("p t j -> p (t j)"), in_=q_planes_ps[:])
         kg2_neg = keep.tile([P, QUADS, 4, T], F32)
         nc.scalar.copy(out=kg2_neg[:], in_=kg_ps[:].rearrange("p (t i a) -> p a i t", t=T, i=4))
         qg2 = keep.tile([P, L, T], F32)
         nc.scalar.copy(out=qg2[:], in_=qg_ps[:].rearrange("p (t j) -> p j t", t=T))
-        q_planes = keep.tile([P, T, L], F32)
-        nc.scalar.copy(out=q_planes[:].rearrange("p t j -> p (t j)"), in_=q_planes_ps[:])
         kg1_rows = kg1[:].rearrange("p a i t -> p (a i) t")
         kg2_rows = kg2_neg[:].rearrange("p a i t -> p (a i) t")
         q_sb = keep.tile([P, L, T], F32)
@@ -221,9 +249,9 @@ def tile_esmfoldsequencetopairproductdifference_w4_kernel(
         def c_tile(tag):
             return work.tile([P, ROWS * L * T], BF16, name=tag, tag=tag, align_bytes=64)
 
-        def scalar_pairs(n, r0, is_diff):
+        def scalar_pairs(n, r0, is_diff, rows=2):
             pairs = work.tile([P, 2, 2, L, 2], BF16, name="pairs", tag="pairs", bufs=3)
-            for r in range(2):
+            for r in range(rows):
                 for t in range(T):
                     dst = pairs[:, r, t // 2, :, t % 2]
                     if is_diff:
@@ -243,10 +271,11 @@ def tile_esmfoldsequencetopairproductdifference_w4_kernel(
                         )
             return pairs
 
-        def scalar_join(pairs, c, r0):
+        def scalar_join(pairs, c, r0, rows=2):
+            words = pairs[:].rearrange("p r u j e -> p (r u j e)").bitcast(F32)
             nc.scalar.copy(
-                out=c[:, r0 * L * T : (r0 + 2) * L * T].bitcast(F32).rearrange("p (r j u) -> p r j u", r=2, u=2),
-                in_=pairs[:].rearrange("p r u j e -> p (r u j e)").bitcast(F32).rearrange("p (r u j) -> p r j u", r=2, u=2),
+                out=c[:, r0 * L * T : (r0 + rows) * L * T].bitcast(F32).rearrange("p (r j u) -> p r j u", r=rows, u=2),
+                in_=words.rearrange("p (r u j) -> p r j u", r=2, u=2)[:, 0:rows, :, :],
             )
 
         def vector_product(n, c, rows, cols):
@@ -259,9 +288,8 @@ def tile_esmfoldsequencetopairproductdifference_w4_kernel(
             )
 
         def diff_tile(dst, a, b):
-            xk = xk_early[:, a - 2, :] if a < EARLY else xk_late[:, a - EARLY, :]
-            nc.tensor.matmul(dst, lhsT=xq[:, b, :], rhs=ident[:], start=True, stop=False, is_transpose=True)
-            nc.tensor.matmul(dst, lhsT=xk, rhs=ident[:], start=False, stop=True, is_transpose=True)
+            nc.tensor.matmul(dst, lhsT=xq[b], rhs=ident[:], start=True, stop=False, is_transpose=True)
+            nc.tensor.matmul(dst, lhsT=xk[a], rhs=ident[:], start=False, stop=True, is_transpose=True)
 
         def diff_bank(n, c, idx):
             bank = spare_bank()
@@ -327,7 +355,13 @@ def tile_esmfoldsequencetopairproductdifference_w4_kernel(
         c_diff = {0: c_tile("c_diff"), 1: c_tile("c_diff")}
         vector_product(0, c_prod[0], ROWS, L)
         vector_product(1, c_prod[1], SHARED_ROWS, L)
-        gpsimd_part(c_diff[0], ALU.add, qg2, kg2_rows, 0, 4, ROWS, 0)
+        nc.vector.tensor_tensor(
+            out=c_diff[0][:, 4 * L * T : 5 * L * T].rearrange("p (j t) -> p j t", t=T),
+            in0=qg_ps[:].rearrange("p (t j) -> p j t", t=T),
+            in1=kg2_rows[:, 4:5, :].to_broadcast([P, L, T]),
+            op=ALU.add,
+        )
+        gpsimd_part(c_diff[0], ALU.add, qg2, kg2_rows, 0, 5, ROWS, 0)
         gpsimd_part(c_diff[1], ALU.add, qg2, kg2_rows, 1, 0, ROWS, DIFF_J)
         first = scalar_pairs(0, 0, True)
         second = scalar_pairs(0, 2, True)
@@ -335,9 +369,9 @@ def tile_esmfoldsequencetopairproductdifference_w4_kernel(
         nc.scalar.copy(out=q_sb[:], in_=q_planes_ps[:].rearrange("p (t j) -> p j t", t=T))
         scalar_join(second, c_diff[0], 2)
         pairs = scalar_pairs(1, ROWS - SCALAR_ROWS, False)
-        diff_bank(1, c_diff[1], 0)
+        diff_bank(1, c_diff[1], 1)
         scalar_join(pairs, c_prod[1], ROWS - SCALAR_ROWS)
-        for idx in range(1, 7):
+        for idx in (4, 2, 5, 3, 6, 0):
             diff_bank(1, c_diff[1], idx)
         prod_q = code_tiles("prod")
         diff_q = code_tiles("diff")

from contextlib import ExitStack

import concourse.mybir as mybir
from concourse.masks import make_identity

L, D, F, C = 128, 1024, 512, 128
FLOPS = 2 * L * D * 2 * F + 2 * L * L * 2 * F * C

F32 = mybir.dt.float32
BF16 = mybir.dt.bfloat16
I32 = mybir.dt.int32
U32 = mybir.dt.uint32
U8 = mybir.dt.uint8
FP8 = mybir.dt.float8_e4m3fn
FP8X4 = mybir.dt.float8_e4m3fn_x4
FP4X4 = mybir.dt.float4_e2m1fn_x4
ALU = mybir.AluOpType
ACT = mybir.ActivationFunctionType

P = 128
T = 4
BANK = 512
QUADS = 32
GROUPS = 16
ROWS = 8
SCALAR_ROWS = 2
SHARED_ROWS = ROWS - SCALAR_ROWS
PROD_J = 96
DIFF_J = 104
TILES = DIFF_J // 8
K_CUTS = (2, 4, 12, QUADS)
Q_CUTS = (0, 4, TILES)


def tile_esmfoldsequencetopairproductdifference_w4_kernel(
    tc, s_bytes, s_scale, w1_words, w1_scales, b1, g, wo_words, wo_scales, bo, out
):
    nc = tc.nc
    with ExitStack() as ctx:
        keep = ctx.enter_context(tc.tile_pool(name="keep", bufs=1))
        work = ctx.enter_context(tc.tile_pool(name="work", bufs=2))
        psum = ctx.enter_context(tc.psum_pool(name="psum", bufs=1))
        ctx.enter_context(tc.manual_schedule())

        def spare_bank():
            return psum.tile([P, BANK], F32, name="spare", tag="spare", bufs=5)

        w1_sc = keep.tile([P, 2, 2 * F], U8, align_bytes=64)
        wo_sc = keep.tile([P, 2, C], U8, align_bytes=64)
        nc.vector.memset(w1_sc[:].bitcast(I32), 0)
        nc.vector.memset(wo_sc[:].bitcast(I32), 0)
        ident = keep.tile([P, P], F32)
        make_identity(nc, ident[:])
        ident_bf = keep.tile([P, P], BF16)
        nc.vector.tensor_copy(out=ident_bf[:], in_=ident[:])
        b1_raw = keep.tile([P, 2, T], BF16)
        nc.scalar.dma_start(out=b1_raw[:], in_=b1.rearrange("(h p t) -> p h t", h=2, t=T))
        g_raw = keep.tile([P, 2, T], BF16)
        nc.scalar.dma_start(out=g_raw[:], in_=g.rearrange("(h p t) -> p h t", h=2, t=T))

        s_raw = keep.tile([P, D], U8)
        nc.sync.dma_start(out=s_raw[:], in_=s_bytes)
        s_sc = keep.tile([P, 2, T], F32)
        nc.sync.dma_start(out=s_sc[:], in_=s_scale.rearrange("o (g p t) -> p (o g) t", p=P, t=T))
        w1_w = [keep.tile([P, 2, 2 * F], U8, align_bytes=64, name="w1_w%d" % half) for half in range(2)]
        w1_src = w1_words.rearrange("g p n -> p g n")

        def load_w1(half):
            nc.sync.dma_start(
                out=w1_w[half][:].bitcast(I32), in_=w1_src[:, :, half * 2 * F : (half + 1) * 2 * F].bitcast(I32)
            )

        load_w1(1)
        for q in range(4):
            nc.sync.dma_start(
                out=w1_sc[32 * q : 32 * q + 4, :, :].bitcast(I32),
                in_=w1_scales[:, 4 * q : 4 * q + 4, :].rearrange("g r n -> r g n").bitcast(I32),
            )
        load_w1(0)
        wo_w = keep.tile([P, 2, 2 * C], U8, align_bytes=64)
        nc.sync.dma_start(out=wo_w[:].bitcast(I32), in_=wo_words.rearrange("g p n -> p g n").bitcast(I32))
        for q in range(4):
            nc.sync.dma_start(
                out=wo_sc[32 * q : 32 * q + 4, :, :].bitcast(I32),
                in_=wo_scales[:, 4 * q : 4 * q + 4, :].rearrange("g r n -> r g n").bitcast(I32),
            )
        bo_all = keep.tile([P, C], BF16)
        nc.sync.dma_start(out=bo_all[:], in_=bo.partition_broadcast(P))

        g_col = keep.tile([P, 2, T], F32)
        nc.scalar.activation(out=g_col[:], in_=g_raw[:], func=ACT.Copy)

        def spread(col):
            bank = spare_bank()
            for t in range(T):
                nc.tensor.matmul(
                    bank[:, t * P : (t + 1) * P],
                    lhsT=col[:, t : t + 1].to_broadcast([P, P]),
                    rhs=ident_bf[:],
                    start=True,
                    stop=True,
                )
            return bank

        def emptied(bank, name, scale):
            wide = keep.tile([P, T, P], F32, name=name)
            nc.scalar.activation(out=wide[:].rearrange("n t p -> n (t p)"), in_=bank[:], func=ACT.Copy, scale=scale)
            return wide

        b1_k = emptied(spread(b1_raw[:, 1, :]), "b1_k", 1.0)
        b1_q = emptied(spread(b1_raw[:, 0, :]), "b1_q", 1.0)

        s_turned = []
        for gi in range(2):
            s_wide = keep.tile([P, BANK], BF16, name="s_wide%d" % gi)
            nc.vector.tensor_copy(out=s_wide[:], in_=s_raw[:, gi * BANK : (gi + 1) * BANK].bitcast(FP8))
            bank = spare_bank()
            for u in range(2):
                nc.tensor.transpose(bank[:, u * P : (u + 1) * P], s_wide[:].bitcast(F32)[:, u:256:2], ident[:])
            s_turned.append(bank)
        g2_ps = spread(g_raw[:, 1, :])
        g2_neg = emptied(g2_ps, "g2_neg", -1.0)
        g2_all = emptied(g2_ps, "g2_all", 1.0)
        s_in = keep.tile([P, 2, L * T], BF16, align_bytes=64)
        for gi in range(2):
            nc.vector.tensor_tensor(
                out=s_in[:, gi, :].rearrange("p (n u e) -> p n u e", u=2, e=2),
                in0=s_turned[gi][:, 0:256].bitcast(BF16).rearrange("p (u n e) -> p n u e", u=2, e=2),
                in1=s_sc[:, gi, :].rearrange("p (u e) -> p u e", u=2).unsqueeze(1).to_broadcast([P, L, 2, 2]),
                op=ALU.mult,
            )
        s_codes = keep.tile([P, 2 * L], U32, align_bytes=64)
        s_scales = keep.tile([P, 2 * L], U8, align_bytes=64)
        for gi in range(2):
            nc.vector.quantize_mx(
                out=s_codes[:, gi * L : (gi + 1) * L].bitcast(FP8X4),
                scales=s_scales[:, gi * L : (gi + 1) * L],
                in_=s_in[:, gi, :],
            )

        h_sb = []
        for half, bias in ((1, b1_k), (0, b1_q)):
            h_ps = spare_bank()
            for gi in range(2):
                nc.tensor.matmul_mx(
                    out=h_ps[:],
                    lhsT=s_codes[:, gi * L : (gi + 1) * L].bitcast(FP8X4),
                    lhsT_scale=s_scales[:, gi * L : (gi + 1) * L],
                    rhs=w1_w[half][:, gi, :].bitcast(FP4X4),
                    rhs_scale=w1_sc[:, gi, half * F : (half + 1) * F],
                    start=(gi == 0),
                    stop=(gi == 1),
                )
            h_half = keep.tile([P, T, P], F32, name="h%d" % half)
            nc.vector.tensor_tensor(
                out=h_half[:],
                in0=h_ps[:].rearrange("n (p t) -> n t p", t=T),
                in1=bias[:],
                op=ALU.add,
            )
            h_sb.append(h_half)
        k_tok, q_tok = h_sb

        kg_tok = keep.tile([P, T, P], F32)
        nc.gpsimd.tensor_tensor(out=kg_tok[:], in0=k_tok[:], in1=g2_neg[:], op=ALU.mult)

        def turn(tok, bank_view):
            for t in range(T):
                nc.tensor.transpose(bank_view[:, t, :], tok[:, t, :], ident[:])

        def turned(tok):
            bank = spare_bank()
            turn(tok, bank[:].rearrange("p (t n) -> p t n", t=T))
            return bank

        k_ps = turned(k_tok)
        kg1 = keep.tile([P, QUADS, 4, T], F32)
        nc.vector.tensor_tensor(
            out=kg1[:],
            in0=k_ps[:].rearrange("p (t i a) -> p a i t", t=T, i=4),
            in1=g_col[:, 0, :].unsqueeze(1).unsqueeze(1).to_broadcast([P, QUADS, 4, T]),
            op=ALU.mult,
        )
        qg_tok = keep.tile([P, T, P], F32)
        nc.vector.tensor_tensor(out=qg_tok[:], in0=q_tok[:], in1=g2_all[:], op=ALU.mult)

        flat = out.rearrange("i j c -> (i j c)")
        row = L * C
        k_park = flat[56 * row : 64 * row]
        q_park = flat[28 * row : 32 * row]
        for cp in range(2):
            nc.sync.dma_start(
                out=k_park[cp * 4 * row : (cp + 1) * 4 * row].rearrange("(t n p) -> n t p", t=T, p=P), in_=kg_tok[:]
            )
        nc.sync.dma_start(out=q_park.rearrange("(n t p) -> n t p", t=T, p=P), in_=qg_tok[:])

        k_rows = k_park.rearrange("(r a p) -> r a p", r=32, p=P)
        q_rows = q_park.rearrange("(b r p) -> r b p", r=32, p=P)
        xk = {}
        xq = {}

        def load_k(piece):
            a0, a1 = K_CUTS[piece], K_CUTS[piece + 1]
            tiles = keep.tile([P, a1 - a0, P], F32, name="xk%d" % piece)
            for jh in (0, 2, 1, 3):
                nc.sync.dma_start(out=tiles[32 * jh : 32 * jh + 32, :, :], in_=k_rows[:, a0:a1, :])
            for a in range(a0, a1):
                xk[a] = tiles[:, a - a0, :]

        def load_q(piece):
            b0, b1_ = Q_CUTS[piece], Q_CUTS[piece + 1]
            tiles = keep.tile([P, b1_ - b0, P], F32, name="xq%d" % piece)
            for ii in range(4):
                nc.sync.dma_start(out=tiles[ii:P:4, :, :], in_=q_rows[:, b0:b1_, :])
            for b in range(b0, b1_):
                xq[b] = tiles[:, b - b0, :]

        load_k(0)
        load_q(0)
        load_q(1)
        load_k(1)
        load_k(2)

        q_ps = psum.tile([P, BANK], F32, tag="q")
        turn(q_tok, q_ps[:].rearrange("p (j t) -> p t j", t=T))
        q_planes_ps = turned(q_tok)
        kg_ps = turned(kg_tok)
        qg_ps = turned(qg_tok)

        q_planes = keep.tile([P, T, L], F32)
        nc.scalar.copy(out=q_planes[:].rearrange("p t j -> p (t j)"), in_=q_planes_ps[:])
        kg2_neg = keep.tile([P, QUADS, 4, T], F32)
        nc.scalar.copy(out=kg2_neg[:], in_=kg_ps[:].rearrange("p (t i a) -> p a i t", t=T, i=4))
        qg2 = keep.tile([P, L, T], F32)
        nc.scalar.copy(out=qg2[:], in_=qg_ps[:].rearrange("p (t j) -> p j t", t=T))
        kg1_rows = kg1[:].rearrange("p a i t -> p (a i) t")
        kg2_rows = kg2_neg[:].rearrange("p a i t -> p (a i) t")
        q_sb = keep.tile([P, L, T], F32)

        def gpsimd_part(c, op, q_side, k_rows_side, n, r0, r1, j0):
            shape = [P, r1 - r0, L - j0, T]
            nc.gpsimd.tensor_tensor(
                out=c[:].rearrange("p (r j t) -> p r j t", j=L, t=T)[:, r0:r1, j0:L, :],
                in0=q_side[:, j0:L, :].unsqueeze(1).to_broadcast(shape),
                in1=k_rows_side[:, ROWS * n + r0 : ROWS * n + r1, :].unsqueeze(2).to_broadcast(shape),
                op=op,
            )

        def c_tile(tag):
            return work.tile([P, ROWS * L * T], BF16, name=tag, tag=tag, align_bytes=64)

        def scalar_pairs(n, r0, is_diff, rows=2):
            pairs = work.tile([P, 2, 2, L, 2], BF16, name="pairs", tag="pairs", bufs=3)
            for r in range(rows):
                for t in range(T):
                    dst = pairs[:, r, t // 2, :, t % 2]
                    if is_diff:
                        nc.scalar.activation(
                            out=dst,
                            in_=q_planes[:, t, :],
                            func=ACT.Identity,
                            scale=g_col[:, 1, t : t + 1],
                            bias=kg2_rows[:, r0 + r, t : t + 1],
                        )
                    else:
                        nc.scalar.activation(
                            out=dst,
                            in_=q_planes[:, t, :],
                            func=ACT.Copy,
                            scale=kg1_rows[:, ROWS * n + r0 + r, t : t + 1],
                        )
            return pairs

        def scalar_join(pairs, c, r0, rows=2):
            words = pairs[:].rearrange("p r u j e -> p (r u j e)").bitcast(F32)
            nc.scalar.copy(
                out=c[:, r0 * L * T : (r0 + rows) * L * T].bitcast(F32).rearrange("p (r j u) -> p r j u", r=rows, u=2),
                in_=words.rearrange("p (r u j) -> p r j u", r=2, u=2)[:, 0:rows, :, :],
            )

        def vector_product(n, c, rows, cols):
            shape = [P, rows, cols, T]
            nc.vector.tensor_tensor(
                out=c[:].rearrange("p (r j t) -> p r j t", j=L, t=T)[:, 0:rows, 0:cols, :],
                in0=q_ps[:].rearrange("p (j t) -> p j t", t=T)[:, 0:cols, :].unsqueeze(1).to_broadcast(shape),
                in1=kg1_rows[:, ROWS * n : ROWS * n + rows, :].unsqueeze(2).to_broadcast(shape),
                op=ALU.mult,
            )

        def diff_tile(dst, a, b):
            nc.tensor.matmul(dst, lhsT=xq[b], rhs=ident[:], start=True, stop=False, is_transpose=True)
            nc.tensor.matmul(dst, lhsT=xk[a], rhs=ident[:], start=False, stop=True, is_transpose=True)

        def diff_bank(n, c, idx):
            bank = spare_bank()
            c_rows = c[:].rearrange("p (a i j t) -> p a i j t", i=4, j=L, t=T)
            if idx > 0:
                a2, beta = divmod(idx - 1, 3)
                for bb in range(4):
                    diff_tile(bank[:, bb * P : (bb + 1) * P], 2 * n + a2, 4 * beta + bb)
                nc.scalar.copy(
                    out=c_rows[:, a2, :, 32 * beta : 32 * beta + 32, :],
                    in_=bank[:].rearrange("p (j t i) -> p i j t", t=T, i=4),
                )
            else:
                for a2 in range(2):
                    diff_tile(bank[:, a2 * P : (a2 + 1) * P], 2 * n + a2, TILES - 1)
                nc.scalar.copy(
                    out=c_rows[:, :, :, 96:DIFF_J, :],
                    in_=bank[:, 0 : 2 * P].rearrange("p (a j t i) -> p a i j t", a=2, t=T, i=4),
                )

        def code_tiles(tag):
            codes = work.tile([P, ROWS * L], U32, name=tag + "_codes", tag=tag + "_codes", align_bytes=64)
            scales = work.tile([P, ROWS * L], U8, name=tag + "_scales", tag=tag + "_scales", align_bytes=64)
            return codes, scales

        def quantise(c, tiles, r0, r1):
            nc.vector.quantize_mx(
                out=tiles[0][:, r0 * L : r1 * L].bitcast(FP8X4),
                scales=tiles[1][:, r0 * L : r1 * L],
                in_=c[:, r0 * L * T : r1 * L * T],
            )

        def project(prod, diff, a2, bank):
            for ii in range(4):
                cols = slice((4 * a2 + ii) * L, (4 * a2 + ii + 1) * L)
                for gi, tiles in enumerate((prod, diff)):
                    nc.tensor.matmul_mx(
                        out=bank[:, ii * C : (ii + 1) * C],
                        lhsT=tiles[0][:, cols].bitcast(FP8X4),
                        lhsT_scale=tiles[1][:, cols],
                        rhs=wo_w[:, gi, :].bitcast(FP4X4),
                        rhs_scale=wo_sc[:, gi, :],
                        start=(gi == 0),
                        stop=(gi == 1),
                    )

        out_rows = out.rearrange("(i a) j c -> a j i c", a=QUADS)

        def finish(a, bank):
            res = work.tile([P, 4, C], F32, name="res", tag="res", bufs=4)
            nc.vector.tensor_tensor(
                out=res[:],
                in0=bank[:].rearrange("p (i c) -> p i c", i=4),
                in1=bo_all[:].unsqueeze(1).to_broadcast([P, 4, C]),
                op=ALU.add,
            )
            nc.sync.dma_start(out=out_rows[a], in_=res[:])

        def out_bank():
            return psum.tile([P, BANK], F32, name="acc", tag="acc", bufs=2)

        c_prod = {0: c_tile("c_prod"), 1: c_tile("c_prod")}
        c_diff = {0: c_tile("c_diff"), 1: c_tile("c_diff")}
        vector_product(0, c_prod[0], ROWS, L)
        vector_product(1, c_prod[1], SHARED_ROWS, L)
        nc.vector.tensor_tensor(
            out=c_diff[0][:, 4 * L * T : 5 * L * T].rearrange("p (j t) -> p j t", t=T),
            in0=qg_ps[:].rearrange("p (t j) -> p j t", t=T),
            in1=kg2_rows[:, 4:5, :].to_broadcast([P, L, T]),
            op=ALU.add,
        )
        gpsimd_part(c_diff[0], ALU.add, qg2, kg2_rows, 0, 5, ROWS, 0)
        gpsimd_part(c_diff[1], ALU.add, qg2, kg2_rows, 1, 0, ROWS, DIFF_J)
        first = scalar_pairs(0, 0, True)
        second = scalar_pairs(0, 2, True)
        scalar_join(first, c_diff[0], 0)
        nc.scalar.copy(out=q_sb[:], in_=q_planes_ps[:].rearrange("p (t j) -> p j t", t=T))
        scalar_join(second, c_diff[0], 2)
        pairs = scalar_pairs(1, ROWS - SCALAR_ROWS, False)
        diff_bank(1, c_diff[1], 1)
        scalar_join(pairs, c_prod[1], ROWS - SCALAR_ROWS)
        for idx in (4, 2, 5, 3, 6, 0):
            diff_bank(1, c_diff[1], idx)
        prod_q = code_tiles("prod")
        diff_q = code_tiles("diff")
        quantise(c_prod[0], prod_q, 0, ROWS)
        quantise(c_diff[0], diff_q, 0, ROWS)

        for n in range(1, GROUPS - 1):
            banks = [out_bank(), out_bank()]
            for a2 in range(2):
                project(prod_q, diff_q, a2, banks[a2])
            c_prod[n + 1] = c_tile("c_prod")
            c_diff[n + 1] = c_tile("c_diff")
            gpsimd_part(c_prod[n + 1], ALU.mult, q_sb, kg1_rows, n + 1, 0, SHARED_ROWS, PROD_J)
            gpsimd_part(c_diff[n + 1], ALU.add, qg2, kg2_rows, n + 1, 0, ROWS, DIFF_J)
            pairs = scalar_pairs(n + 1, ROWS - SCALAR_ROWS, False)
            diff_bank(n + 1, c_diff[n + 1], 0)
            scalar_join(pairs, c_prod[n + 1], ROWS - SCALAR_ROWS)
            for idx in range(1, 7):
                diff_bank(n + 1, c_diff[n + 1], idx)
            vector_product(n + 1, c_prod[n + 1], SHARED_ROWS, PROD_J)
            for a2 in range(2):
                finish(2 * (n - 1) + a2, banks[a2])
            prod_q = code_tiles("prod")
            diff_q = code_tiles("diff")
            quantise(c_prod[n], prod_q, 0, ROWS)
            quantise(c_diff[n], diff_q, 0, ROWS)

        n = GROUPS - 1
        banks = [out_bank(), out_bank()]
        for a2 in range(2):
            project(prod_q, diff_q, a2, banks[a2])
        prod_q = code_tiles("prod")
        diff_q = code_tiles("diff")
        quantise(c_prod[n], prod_q, 0, ROWS)
        for a2 in range(2):
            quantise(c_diff[n], diff_q, 4 * a2, 4 * a2 + 4)
        for a2 in range(2):
            finish(2 * (n - 1) + a2, banks[a2])
        for a2 in range(2):
            bank = spare_bank()
            project(prod_q, diff_q, a2, bank)
            finish(2 * n + a2, bank)
